import numpy as np
import ml_dtypes


def mxq(x, axis, fmt="e4m3"):
    dtype, down = {"e4m3": (ml_dtypes.float8_e4m3fn, 7), "e5m2": (ml_dtypes.float8_e5m2, 14)}[fmt]
    v = np.moveaxis(np.asarray(x, np.float32).astype(ml_dtypes.bfloat16).astype(np.float64), axis, -1)
    blocks = v.reshape(v.shape[:-1] + (-1, 32))
    amax = np.abs(blocks).max(-1, keepdims=True)
    byte = np.maximum(np.where(amax > 0, np.frexp(amax)[1] - 1 + 127, 0) - down, 1)
    scale = np.exp2(byte - 127.0)
    codes = (blocks / scale).astype(np.float32).astype(dtype).astype(np.float64)
    return np.moveaxis((codes * scale).reshape(v.shape), -1, axis)


WIDE = False


def mx_kscale(k):
    if not WIDE:
        return np.ones(k)
    levels = np.array([10, -10, 5, -5, 0])
    if k % 512:
        return np.exp2(np.random.permutation(np.resize(levels, k // 32))).repeat(32)
    a = np.empty((k // 512, 16))
    for p in range(k // 512):
        a[p, :8] = np.random.permutation(np.resize(levels, 8))
        for g in range(8):
            far = levels[np.abs(levels - a[p, g]) >= 10]
            a[p, g + 8] = far[np.random.randint(len(far))]
    return np.exp2(a.ravel()).repeat(32)


def f64(x):
    return np.asarray(x).astype(np.float64)


def striped(idx):
    return np.tile(idx.reshape(-1, 16).T, (8, 1)).astype(np.uint16)


def unstriped(offs):
    return offs[:16].T.reshape(-1).astype(np.int64)


def pack_weight(w):
    k, n = w.shape
    w = f64(np.asarray(w, np.float32).astype(ml_dtypes.bfloat16)).reshape(k // 32, 32, n)
    amax = np.abs(w).max(1)
    byte = np.clip(np.where(amax > 0, np.frexp(amax)[1] - 1 + 127 - 7, 1), 1, 254)
    scaled = (w * np.exp2(127.0 - byte)[:, None, :]).reshape(k, n).astype(np.float32)
    words = np.ascontiguousarray(scaled.reshape(k // 512, 128, 4, n).transpose(0, 1, 3, 2)).astype(ml_dtypes.float8_e4m3fn).view(np.uint8)
    return words, np.ascontiguousarray(byte.astype(np.uint8).reshape(k // 512, 16, n))


def unpack_weight(words, scales):
    g, p, n, _ = words.shape
    vals = np.ascontiguousarray(words).view(ml_dtypes.float8_e4m3fn).astype(np.float64) * np.repeat(np.exp2(scales.astype(np.float64) - 127.0), 8, axis=1)[..., None]
    return vals.transpose(0, 1, 3, 2).reshape(g * 512, n)


K, T, E, C, N = 1536, 512, 8, 128, 512


def by_expert(wq, xq):
    return np.concatenate([wq[e].T @ xq[:, e * C:(e + 1) * C] for e in range(E)], axis=1)


def setup_inputs():
    n = np.random.standard_normal
    s = mx_kscale(K)[:, None]
    first = np.random.permutation(np.repeat(np.arange(E), T // E))
    second = (first + 1 + np.random.permutation(np.repeat(np.arange(E - 1), -(-T // (E - 1)))[:T])) % E
    while np.bincount(second, minlength=E).max() != T // E:
        load = np.bincount(second, minlength=E); hi, lo = int(load.argmax()), int(load.argmin())
        t = np.flatnonzero((second == hi) & (first != lo))[0]; second[t] = lo
    slot_token = np.empty(E * C, np.int64); pos = np.empty((2, T), np.int64); fill = np.zeros(E, np.int64)
    place = np.stack([np.random.permutation(C) for _ in range(E)])
    for r, deal in enumerate((first, second)):
        for t in np.random.permutation(T):
            e = deal[t]; j = e * C + place[e, fill[e]]; fill[e] += 1; slot_token[j] = t; pos[r, t] = j
    g = np.random.uniform(0.2, 0.8, T)
    packed = [pack_weight(m) for m in n((E, K, N)) / np.sqrt(K) / s[None]]
    return {
        "xT": (n((K, T)) * s).astype(np.float32),
        "w_words": np.stack([m[0] for m in packed]),
        "w_scales": np.stack([m[1] for m in packed]),
        "gate": np.stack([np.tile(g, (N, 1)), np.tile(1.0 - g, (N, 1))]).astype(np.float32),
        "offs": striped(slot_token),
        "pos1": striped(pos[0]),
        "pos2": striped(pos[1]),
    }


def reference(xT, w_words, w_scales, gate, offs, pos1, pos2):
    idx = unstriped(offs)
    xq = mxq(f64(xT)[:, idx], 0, "e4m3")
    w = np.stack([unpack_weight(w_words[e], w_scales[e]) for e in range(E)])
    y = by_expert(w, xq)
    return f64(gate[0]) * y[:, unstriped(pos1)] + f64(gate[1]) * y[:, unstriped(pos2)]

@@ -1,0 +1,165 @@
+from contextlib import ExitStack
+
+import concourse.mybir as mybir
+from concourse.masks import make_identity
+
+K, T, E, C, N = 1536, 512, 8, 128, 512
+F32 = mybir.dt.float32
+BF16 = mybir.dt.bfloat16
+I32 = mybir.dt.int32
+U32 = mybir.dt.uint32
+U16 = mybir.dt.uint16
+U8 = mybir.dt.uint8
+FP8X4 = mybir.dt.float8_e4m3fn_x4
+MULT = mybir.AluOpType.mult
+ADD = mybir.AluOpType.add
+
+P = 128
+PACK = 4
+A = K // (P * PACK)
+SLOTS = E * C
+NB = N // P
+FULL = 4
+PAIR = 2
+VECTOR_BLOCKS = (88, 0, 0)
+CUTS = [(0, 384), (384, 768), (768, 1024)]
+
+FLOPS = 2 * K * N * SLOTS
+BYTES = 4 * K * T + K * N * E + K * N * E // 32 + 4 * 2 * T + 2 * (8 * SLOTS + 2 * 8 * T) + 4 * N * T
+
+
+def tile_routed_moe_kernel(tc, xT, w_words, w_scales, gate, offs, pos1, pos2, out):
+    nc = tc.nc
+    with ExitStack() as ctx:
+        keep = ctx.enter_context(tc.tile_pool(name="keep", bufs=1))
+        ring = ctx.enter_context(tc.tile_pool(name="ring", bufs=2))
+        psum = ctx.enter_context(tc.psum_pool(name="psum", bufs=8))
+
+        offs_t = keep.tile([P, SLOTS // 16], U16, name="offs_t")
+        pos1_t = keep.tile([P, T // 16], U16, name="pos1_t")
+        pos2_t = keep.tile([P, T // 16], U16, name="pos2_t")
+
+        xs = keep.tile([P, T], U8, name="xs", align_bytes=64)
+        nc.gpsimd.memset(xs[:], 0)
+        wsc = keep.tile([P, E, N], U8, name="wsc", align_bytes=64)
+        nc.vector.memset(wsc[:].rearrange("p e n -> p (e n)").bitcast(I32), 0)
+        grow = keep.tile([P, 2, T], F32, name="grow")
+        nc.gpsimd.memset(grow[:], 0.0)
+        ones = keep.tile([P, P], F32, name="ones")
+        nc.gpsimd.memset(ones[:], 1.0)
+
+        ident = keep.tile([P, P], F32, name="ident")
+        make_identity(nc, ident[:])
+
+        raws = []
+        for a in range(A):
+            raw = keep.tile([P, PACK, T], F32, name=f"raw{a}")
+            raws.append(raw)
+        xv = xT.rearrange("(a p j) w -> a p j w", p=P, j=PACK)
+        nc.sync.dma_start(raws[0][:], xv[0])
+        nc.sync.dma_start(offs_t[:], offs)
+        nc.sync.dma_start(raws[1][:], xv[1])
+        nc.sync.dma_start(grow[0:1, :, :], gate[:, 0:1, :].rearrange("g o t -> o g t"))
+        nc.sync.dma_start(raws[2][:], xv[2])
+        for a in range(A):
+            for r in range(4):
+                nc.sync.dma_start(
+                    wsc[4 * a + r : P : 32, :, :].bitcast(I32),
+                    w_scales[:, a, r:16:4, :].bitcast(I32).rearrange("e q n -> q e n"),
+                )
+        wfull = []
+        for e in range(FULL):
+            w = keep.tile([P, A, N], U32, name=f"wfull{e}", align_bytes=64)
+            nc.sync.dma_start(w[:].bitcast(I32), w_words[e].rearrange("a p n r -> p a (n r)").bitcast(I32))
+            wfull.append(w)
+        nc.sync.dma_start(pos1_t[:], pos1)
+        nc.sync.dma_start(pos2_t[:], pos2)
+        wpart = {}
+        for nb in range(NB):
+            for e in range(FULL, E, PAIR):
+                w = keep.tile([P, PAIR * A, P], U32, name=f"wpart{nb}_{e}", align_bytes=64)
+                src = w_words[e : e + PAIR, :, :, nb * P : (nb + 1) * P, :]
+                nc.sync.dma_start(w[:].bitcast(I32), src.rearrange("e a p n r -> p (e a) (n r)").bitcast(I32))
+                for i in range(PAIR):
+                    wpart[nb, e + i] = (w, i)
+
+        gates = []
+        for g in range(2):
+            bank = psum.tile([P, T], F32, name=f"gbank{g}", tag="bank")
+            nc.tensor.matmul(bank[:], lhsT=ones[:], rhs=grow[:, g, :], start=True, stop=True)
+            gt = keep.tile([P, T], F32, name=f"gate{g}")
+            nc.scalar.copy(gt[:], bank[:])
+            gates.append(gt)
+
+        xq = []
+        gq = []
+        gs = keep.tile([P, SLOTS], U8, name="gs", align_bytes=64)
+        for a in range(A):
+            g = keep.tile([P, T, PACK], BF16, name=f"grouped{a}", align_bytes=64)
+            dst = g[:].rearrange("p (c i) t -> p c t i", i=4)
+            src = raws[a][:].rearrange("p t (c i) -> p c t i", i=4)
+            cut = VECTOR_BLOCKS[a]
+            if cut:
+                nc.vector.tensor_copy(dst[:, :cut], src[:, :cut])
+            if cut < T // 4:
+                nc.scalar.copy(dst[:, cut:], src[:, cut:])
+            q = keep.tile([P, T], U32, name=f"xq{a}", align_bytes=64)
+            nc.vector.quantize_mx(
+                out=q[:].bitcast(FP8X4), scales=xs[4 * a : P, :], in_=g[:].rearrange("p w j -> p (w j)")
+            )
+            xq.append(q)
+            gathered = keep.tile([P, SLOTS], U32, name=f"gq{a}", align_bytes=64)
+            gq.append(gathered)
+            for lo, hi in CUTS:
+                idx = offs_t[:, lo // 16 : hi // 16]
+                if a == A - 1:
+                    nc.vector.tensor_copy(gs[:, lo:hi], xs[:].indirect(idx))
+                nc.vector.tensor_copy(gathered[:, lo:hi], q[:].indirect(idx))
+
+        sums = {}
+        for nb in range(NB):
+            ysb = keep.tile([P, SLOTS], F32, name=f"y{nb}")
+            sums[nb] = ysb
+
+        def half(nb, h):
+            bank = psum.tile([P, FULL * C], F32, name=f"acc{nb}_{h}", tag="bank")
+            for e in range(h * FULL, (h + 1) * FULL):
+                for a in range(A):
+                    if e < FULL:
+                        lhs = wfull[e][:, a, nb * P : (nb + 1) * P]
+                    else:
+                        w, i = wpart[nb, e]
+                        lhs = w[:, i * A + a, :]
+                    nc.tensor.matmul_mx(
+                        out=bank[:, (e % FULL) * C : (e % FULL + 1) * C],
+                        lhsT=lhs.bitcast(FP8X4),
+                        lhsT_scale=wsc[4 * a : P, e, nb * P : (nb + 1) * P],
+                        rhs=gq[a][:, e * C : (e + 1) * C].bitcast(FP8X4),
+                        rhs_scale=gs[4 * a : P, e * C : (e + 1) * C],
+                        start=(a == 0),
+                        stop=(a == A - 1),
+                    )
+            nc.scalar.copy(sums[nb][:, h * FULL * C : (h + 1) * FULL * C], bank[:])
+
+        def products(nb):
+            prods = []
+            for g, pos in enumerate((pos1_t, pos2_t)):
+                pr = ring.tile([P, T], F32, name=f"prod{g}")
+                nc.vector.tensor_tensor(pr[:], sums[nb][:].indirect(pos[:]), gates[g][:], MULT)
+                prods.append(pr)
+            return prods
+
+        for nb in range(NB):
+            half(nb, 0)
+        for nb in range(NB):
+            half(nb, 1)
+            prods = products(nb)
+            res = ring.tile([P, T], F32, name="res")
+            if nb < NB - 1:
+                total = psum.tile([P, T], F32, name=f"total{nb}", tag="bank")
+                for g in range(2):
+                    nc.tensor.matmul(total[:], lhsT=ident[:], rhs=prods[g][:], start=(g == 0), stop=(g == 1))
+                nc.scalar.copy(res[:], total[:])
+            else:
+                nc.vector.tensor_tensor(res[:], prods[0][:], prods[1][:], ADD)
+            nc.sync.dma_start(out[nb * P : (nb + 1) * P, :], res[:])

@@ -21,7 +21,6 @@ SLOTS = E * C
 NB = N // P
 FULL = 4
 PAIR = 2
-VECTOR_BLOCKS = (88, 0, 0)
 CUTS = [(0, 384), (384, 768), (768, 1024)]
 
 FLOPS = 2 * K * N * SLOTS
@@ -56,7 +55,9 @@ def tile_routed_moe_kernel(tc, xT, w_words, w_scales, gate, offs, pos1, pos2, ou
             raw = keep.tile([P, PACK, T], F32, name=f"raw{a}")
             raws.append(raw)
         xv = xT.rearrange("(a p j) w -> a p j w", p=P, j=PACK)
-        nc.sync.dma_start(raws[0][:], xv[0])
+        H = T // 2
+        for h in range(2):
+            nc.sync.dma_start(raws[0][:, :, h * H : (h + 1) * H], xv[0][:, :, h * H : (h + 1) * H])
         nc.sync.dma_start(offs_t[:], offs)
         nc.sync.dma_start(raws[1][:], xv[1])
         nc.sync.dma_start(grow[0:1, :, :], gate[:, 0:1, :].rearrange("g o t -> o g t"))
@@ -98,15 +99,24 @@ def tile_routed_moe_kernel(tc, xT, w_words, w_scales, gate, offs, pos1, pos2, ou
             g = keep.tile([P, T, PACK], BF16, name=f"grouped{a}", align_bytes=64)
             dst = g[:].rearrange("p (c i) t -> p c t i", i=4)
             src = raws[a][:].rearrange("p t (c i) -> p c t i", i=4)
-            cut = VECTOR_BLOCKS[a]
-            if cut:
-                nc.vector.tensor_copy(dst[:, :cut], src[:, :cut])
-            if cut < T // 4:
-                nc.scalar.copy(dst[:, cut:], src[:, cut:])
             q = keep.tile([P, T], U32, name=f"xq{a}", align_bytes=64)
-            nc.vector.quantize_mx(
-                out=q[:].bitcast(FP8X4), scales=xs[4 * a : P, :], in_=g[:].rearrange("p w j -> p (w j)")
-            )
+
+            def quantise(lo, hi):
+                nc.vector.quantize_mx(
+                    out=q[:, lo:hi].bitcast(FP8X4),
+                    scales=xs[4 * a : P, lo:hi],
+                    in_=g[:, lo:hi, :].rearrange("p w j -> p (w j)"),
+                )
+
+            if a == 0:
+                nc.vector.tensor_copy(dst[:, 0:64], src[:, 0:64])
+                quantise(0, 256)
+                nc.scalar.copy(dst[:, 108:128], src[:, 108:128])
+                nc.vector.tensor_copy(dst[:, 64:108], src[:, 64:108])
+                quantise(256, 512)
+            else:
+                nc.scalar.copy(dst, src)
+                quantise(0, 512)
             xq.append(q)
             gathered = keep.tile([P, SLOTS], U32, name=f"gq{a}", align_bytes=64)
             gq.append(gathered)
@@ -149,10 +159,10 @@ def tile_routed_moe_kernel(tc, xT, w_words, w_scales, gate, offs, pos1, pos2, ou
                 prods.append(pr)
             return prods
 
+        for h in range(2):
+            for nb in range(NB):
+                half(nb, h)
         for nb in range(NB):
-            half(nb, 0)
-        for nb in range(NB):
-            half(nb, 1)
             prods = products(nb)
             res = ring.tile([P, T], F32, name="res")
             if nb < NB - 1:

@@ -1,7 +1,6 @@
 from contextlib import ExitStack
 
 import concourse.mybir as mybir
-from concourse.masks import make_identity
 
 K, T, E, C, N = 1536, 512, 8, 128, 512
 F32 = mybir.dt.float32
@@ -19,9 +18,8 @@ PACK = 4
 A = K // (P * PACK)
 SLOTS = E * C
 NB = N // P
-FULL = 4
-PAIR = 2
-CUTS = [(0, 384), (384, 768), (768, 1024)]
+FULL = 3
+GROUPS = ((0, 3), (3, 6), (6, 8))
 
 FLOPS = 2 * K * N * SLOTS
 BYTES = 4 * K * T + K * N * E + K * N * E // 32 + 4 * 2 * T + 2 * (8 * SLOTS + 2 * 8 * T) + 4 * N * T
@@ -31,24 +29,21 @@ def tile_routed_moe_kernel(tc, xT, w_words, w_scales, gate, offs, pos1, pos2, ou
     nc = tc.nc
     with ExitStack() as ctx:
         keep = ctx.enter_context(tc.tile_pool(name="keep", bufs=1))
-        ring = ctx.enter_context(tc.tile_pool(name="ring", bufs=2))
-        psum = ctx.enter_context(tc.psum_pool(name="psum", bufs=8))
+        ring = ctx.enter_context(tc.tile_pool(name="ring", bufs=4))
+        banks = {}
+        for tag, bufs in (("low", 1), ("even", 1), ("odd", 1), ("gate", 2)):
+            banks[tag] = ctx.enter_context(tc.psum_pool(name=f"psum_{tag}", bufs=bufs))
 
         offs_t = keep.tile([P, SLOTS // 16], U16, name="offs_t")
         pos1_t = keep.tile([P, T // 16], U16, name="pos1_t")
         pos2_t = keep.tile([P, T // 16], U16, name="pos2_t")
 
-        xs = keep.tile([P, T], U8, name="xs", align_bytes=64)
-        nc.gpsimd.memset(xs[:], 0)
         wsc = keep.tile([P, E, N], U8, name="wsc", align_bytes=64)
         nc.vector.memset(wsc[:].rearrange("p e n -> p (e n)").bitcast(I32), 0)
+        xs = keep.tile([P, T], U8, name="xs", align_bytes=64)
+        nc.gpsimd.memset(xs[:], 0)
         grow = keep.tile([P, 2, T], F32, name="grow")
         nc.gpsimd.memset(grow[:], 0.0)
-        ones = keep.tile([P, P], F32, name="ones")
-        nc.gpsimd.memset(ones[:], 1.0)
-
-        ident = keep.tile([P, P], F32, name="ident")
-        make_identity(nc, ident[:])
 
         raws = []
         for a in range(A):
@@ -60,8 +55,8 @@ def tile_routed_moe_kernel(tc, xT, w_words, w_scales, gate, offs, pos1, pos2, ou
             nc.sync.dma_start(raws[0][:, :, h * H : (h + 1) * H], xv[0][:, :, h * H : (h + 1) * H])
         nc.sync.dma_start(offs_t[:], offs)
         nc.sync.dma_start(raws[1][:], xv[1])
-        nc.sync.dma_start(grow[0:1, :, :], gate[:, 0:1, :].rearrange("g o t -> o g t"))
         nc.sync.dma_start(raws[2][:], xv[2])
+        nc.sync.dma_start(grow[0:1, :, :], gate[:, 0:1, :].rearrange("g o t -> o g t"))
         for a in range(A):
             for r in range(4):
                 nc.sync.dma_start(
@@ -73,30 +68,22 @@ def tile_routed_moe_kernel(tc, xT, w_words, w_scales, gate, offs, pos1, pos2, ou
             w = keep.tile([P, A, N], U32, name=f"wfull{e}", align_bytes=64)
             nc.sync.dma_start(w[:].bitcast(I32), w_words[e].rearrange("a p n r -> p a (n r)").bitcast(I32))
             wfull.append(w)
-        nc.sync.dma_start(pos1_t[:], pos1)
-        nc.sync.dma_start(pos2_t[:], pos2)
         wpart = {}
         for nb in range(NB):
-            for e in range(FULL, E, PAIR):
-                w = keep.tile([P, PAIR * A, P], U32, name=f"wpart{nb}_{e}", align_bytes=64)
-                src = w_words[e : e + PAIR, :, :, nb * P : (nb + 1) * P, :]
+            for lo, hi in GROUPS[1:]:
+                w = keep.tile([P, (hi - lo) * A, P], U32, name=f"wpart{nb}_{lo}", align_bytes=64)
+                src = w_words[lo:hi, :, :, nb * P : (nb + 1) * P, :]
                 nc.sync.dma_start(w[:].bitcast(I32), src.rearrange("e a p n r -> p (e a) (n r)").bitcast(I32))
-                for i in range(PAIR):
-                    wpart[nb, e + i] = (w, i)
-
-        gates = []
-        for g in range(2):
-            bank = psum.tile([P, T], F32, name=f"gbank{g}", tag="bank")
-            nc.tensor.matmul(bank[:], lhsT=ones[:], rhs=grow[:, g, :], start=True, stop=True)
-            gt = keep.tile([P, T], F32, name=f"gate{g}")
-            nc.scalar.copy(gt[:], bank[:])
-            gates.append(gt)
+                wpart[nb, lo] = w
+            if nb == 0:
+                nc.sync.dma_start(pos1_t[:], pos1)
+                nc.sync.dma_start(pos2_t[:], pos2)
 
         xq = []
         gq = []
         gs = keep.tile([P, SLOTS], U8, name="gs", align_bytes=64)
         for a in range(A):
-            g = keep.tile([P, T, PACK], BF16, name=f"grouped{a}", align_bytes=64)
+            g = keep.tile([P, T, PACK], BF16, name=f"grouped{a}", tag="late" if a == A - 1 else f"grouped{a}", align_bytes=64)
             dst = g[:].rearrange("p (c i) t -> p c t i", i=4)
             src = raws[a][:].rearrange("p t (c i) -> p c t i", i=4)
             q = keep.tile([P, T], U32, name=f"xq{a}", align_bytes=64)
@@ -111,65 +98,68 @@ def tile_routed_moe_kernel(tc, xT, w_words, w_scales, gate, offs, pos1, pos2, ou
             if a == 0:
                 nc.vector.tensor_copy(dst[:, 0:64], src[:, 0:64])
                 quantise(0, 256)
-                nc.scalar.copy(dst[:, 108:128], src[:, 108:128])
-                nc.vector.tensor_copy(dst[:, 64:108], src[:, 64:108])
+                nc.scalar.copy(dst[:, 104:128], src[:, 104:128])
+                nc.vector.tensor_copy(dst[:, 64:104], src[:, 64:104])
                 quantise(256, 512)
+            elif a == 1:
+                nc.scalar.copy(dst[:, 48:128], src[:, 48:128])
+                nc.vector.tensor_copy(dst[:, 0:48], src[:, 0:48])
+                quantise(0, 512)
             else:
                 nc.scalar.copy(dst, src)
                 quantise(0, 512)
             xq.append(q)
             gathered = keep.tile([P, SLOTS], U32, name=f"gq{a}", align_bytes=64)
             gq.append(gathered)
-            for lo, hi in CUTS:
+            for first, last in GROUPS:
+                lo, hi = first * C, last * C
                 idx = offs_t[:, lo // 16 : hi // 16]
                 if a == A - 1:
                     nc.vector.tensor_copy(gs[:, lo:hi], xs[:].indirect(idx))
                 nc.vector.tensor_copy(gathered[:, lo:hi], q[:].indirect(idx))
 
-        sums = {}
+        ones = keep.tile([P, P], F32, name="ones", tag="late", align_bytes=64)
+        nc.gpsimd.memset(ones[:], 1.0)
+        gates = []
+        for g in range(2):
+            bank = banks["gate"].tile([P, T], F32, name=f"gbank{g}", tag="gate")
+            nc.tensor.matmul(bank[:], lhsT=ones[:], rhs=grow[:, g, :], start=True, stop=True)
+            gt = keep.tile([P, T], F32, name=f"gate{g}")
+            nc.scalar.copy(gt[:], bank[:])
+            gates.append(gt)
+
+        sums = []
         for nb in range(NB):
             ysb = keep.tile([P, SLOTS], F32, name=f"y{nb}")
-            sums[nb] = ysb
+            sums.append(ysb)
 
-        def half(nb, h):
-            bank = psum.tile([P, FULL * C], F32, name=f"acc{nb}_{h}", tag="bank")
-            for e in range(h * FULL, (h + 1) * FULL):
-                for a in range(A):
-                    if e < FULL:
-                        lhs = wfull[e][:, a, nb * P : (nb + 1) * P]
-                    else:
-                        w, i = wpart[nb, e]
-                        lhs = w[:, i * A + a, :]
-                    nc.tensor.matmul_mx(
-                        out=bank[:, (e % FULL) * C : (e % FULL + 1) * C],
-                        lhsT=lhs.bitcast(FP8X4),
-                        lhsT_scale=wsc[4 * a : P, e, nb * P : (nb + 1) * P],
-                        rhs=gq[a][:, e * C : (e + 1) * C].bitcast(FP8X4),
-                        rhs_scale=gs[4 * a : P, e * C : (e + 1) * C],
-                        start=(a == 0),
-                        stop=(a == A - 1),
-                    )
-            nc.scalar.copy(sums[nb][:, h * FULL * C : (h + 1) * FULL * C], bank[:])
+        for nb in range(NB):
+            for i, (first, last) in enumerate(GROUPS):
+                tag = "low" if i == 0 else ("even", "odd")[(nb + i + 1) % 2]
+                bank = banks[tag].tile([P, T], F32, name=f"acc{nb}_{first}", tag=tag)
+                for e in range(first, last):
+                    for a in range(A):
+                        if e < FULL:
+                            lhs = wfull[e][:, a, nb * P : (nb + 1) * P]
+                        else:
+                            lhs = wpart[nb, first][:, (e - first) * A + a, :]
+                        nc.tensor.matmul_mx(
+                            out=bank[:, (e - first) * C : (e - first + 1) * C],
+                            lhsT=lhs.bitcast(FP8X4),
+                            lhsT_scale=wsc[4 * a : P, e, nb * P : (nb + 1) * P],
+                            rhs=gq[a][:, e * C : (e + 1) * C].bitcast(FP8X4),
+                            rhs_scale=gs[4 * a : P, e * C : (e + 1) * C],
+                            start=(a == 0),
+                            stop=(a == A - 1),
+                        )
+                nc.scalar.copy(sums[nb][:, first * C : last * C], bank[:, : (last - first) * C])
 
-        def products(nb):
+        for nb in range(NB):
             prods = []
             for g, pos in enumerate((pos1_t, pos2_t)):
                 pr = ring.tile([P, T], F32, name=f"prod{g}")
                 nc.vector.tensor_tensor(pr[:], sums[nb][:].indirect(pos[:]), gates[g][:], MULT)
                 prods.append(pr)
-            return prods
-
-        for h in range(2):
-            for nb in range(NB):
-                half(nb, h)
-        for nb in range(NB):
-            prods = products(nb)
             res = ring.tile([P, T], F32, name="res")
-            if nb < NB - 1:
-                total = psum.tile([P, T], F32, name=f"total{nb}", tag="bank")
-                for g in range(2):
-                    nc.tensor.matmul(total[:], lhsT=ident[:], rhs=prods[g][:], start=(g == 0), stop=(g == 1))
-                nc.scalar.copy(res[:], total[:])
-            else:
-                nc.vector.tensor_tensor(res[:], prods[0][:], prods[1][:], ADD)
+            nc.vector.tensor_tensor(res[:], prods[0][:], prods[1][:], ADD)
             nc.sync.dma_start(out[nb * P : (nb + 1) * P, :], res[:])

@@ -18,7 +18,8 @@ PACK = 4
 A = K // (P * PACK)
 SLOTS = E * C
 NB = N // P
-FULL = 3
+FULL = 2
+PARTS = ((2, 4), (4, 6), (6, 8))
 GROUPS = ((0, 3), (3, 6), (6, 8))
 
 FLOPS = 2 * K * N * SLOTS
@@ -31,7 +32,7 @@ def tile_routed_moe_kernel(tc, xT, w_words, w_scales, gate, offs, pos1, pos2, ou
         keep = ctx.enter_context(tc.tile_pool(name="keep", bufs=1))
         ring = ctx.enter_context(tc.tile_pool(name="ring", bufs=4))
         banks = {}
-        for tag, bufs in (("low", 1), ("even", 1), ("odd", 1), ("gate", 2)):
+        for tag, bufs in (("low", 2), ("even", 1), ("odd", 1), ("gate", 2), ("extra", 1)):
             banks[tag] = ctx.enter_context(tc.psum_pool(name=f"psum_{tag}", bufs=bufs))
 
         offs_t = keep.tile([P, SLOTS // 16], U16, name="offs_t")
@@ -70,11 +71,12 @@ def tile_routed_moe_kernel(tc, xT, w_words, w_scales, gate, offs, pos1, pos2, ou
             wfull.append(w)
         wpart = {}
         for nb in range(NB):
-            for lo, hi in GROUPS[1:]:
+            for lo, hi in PARTS:
                 w = keep.tile([P, (hi - lo) * A, P], U32, name=f"wpart{nb}_{lo}", align_bytes=64)
                 src = w_words[lo:hi, :, :, nb * P : (nb + 1) * P, :]
                 nc.sync.dma_start(w[:].bitcast(I32), src.rearrange("e a p n r -> p (e a) (n r)").bitcast(I32))
-                wpart[nb, lo] = w
+                for e in range(lo, hi):
+                    wpart[nb, e] = w[:, (e - lo) * A : (e - lo + 1) * A, :]
             if nb == 0:
                 nc.sync.dma_start(pos1_t[:], pos1)
                 nc.sync.dma_start(pos2_t[:], pos2)
@@ -133,33 +135,65 @@ def tile_routed_moe_kernel(tc, xT, w_words, w_scales, gate, offs, pos1, pos2, ou
             ysb = keep.tile([P, SLOTS], F32, name=f"y{nb}")
             sums.append(ysb)
 
-        for nb in range(NB):
+        def one_pass(nb, bank, column, e, a):
+            if e < FULL:
+                lhs = wfull[e][:, a, nb * P : (nb + 1) * P]
+            else:
+                lhs = wpart[nb, e][:, a, :]
+            nc.tensor.matmul_mx(
+                out=bank[:, column : column + C],
+                lhsT=lhs.bitcast(FP8X4),
+                lhsT_scale=wsc[4 * a : P, e, nb * P : (nb + 1) * P],
+                rhs=gq[a][:, e * C : (e + 1) * C].bitcast(FP8X4),
+                rhs_scale=gs[4 * a : P, e * C : (e + 1) * C],
+                start=(a == 0),
+                stop=(a == A - 1),
+            )
+
+        def open_bank(tag, name):
+            bank = banks[tag].tile([P, T], F32, name=name, tag=tag)
+            return bank
+
+        def multiply(nb):
             for i, (first, last) in enumerate(GROUPS):
                 tag = "low" if i == 0 else ("even", "odd")[(nb + i + 1) % 2]
-                bank = banks[tag].tile([P, T], F32, name=f"acc{nb}_{first}", tag=tag)
+                bank = open_bank(tag, f"acc{nb}_{first}")
+                if nb == 0 and i == 2:
+                    extra = open_bank("extra", "extra")
+                    for a in range(A):
+                        one_pass(nb, bank, 0, 6, a)
+                        one_pass(nb, extra, 0, 7, a)
+                    nc.scalar.copy(sums[nb][:, 6 * C : 7 * C], bank[:, :C])
+                    nc.vector.tensor_copy(sums[nb][:, 7 * C :], extra[:, :C])
+                    continue
                 for e in range(first, last):
                     for a in range(A):
-                        if e < FULL:
-                            lhs = wfull[e][:, a, nb * P : (nb + 1) * P]
-                        else:
-                            lhs = wpart[nb, first][:, (e - first) * A + a, :]
-                        nc.tensor.matmul_mx(
-                            out=bank[:, (e - first) * C : (e - first + 1) * C],
-                            lhsT=lhs.bitcast(FP8X4),
-                            lhsT_scale=wsc[4 * a : P, e, nb * P : (nb + 1) * P],
-                            rhs=gq[a][:, e * C : (e + 1) * C].bitcast(FP8X4),
-                            rhs_scale=gs[4 * a : P, e * C : (e + 1) * C],
-                            start=(a == 0),
-                            stop=(a == A - 1),
-                        )
+                        one_pass(nb, bank, (e - first) * C, e, a)
                 nc.scalar.copy(sums[nb][:, first * C : last * C], bank[:, : (last - first) * C])
 
+        def product(nb, g, lo=0, hi=T):
+            pr = ring.tile([P, hi - lo], F32, name=f"prod{nb}_{g}_{lo}", tag=f"prod{g}")
+            idx = (pos1_t, pos2_t)[g][:, lo // 16 : hi // 16]
+            nc.vector.tensor_tensor(pr[:], sums[nb][:].indirect(idx), gates[g][:, lo:hi], MULT)
+            return pr
+
+        def add(nb, a, b, lo=0, hi=T):
+            res = ring.tile([P, hi - lo], F32, name=f"res{nb}_{lo}", tag="res")
+            nc.vector.tensor_tensor(res[:], a, b, ADD)
+            nc.sync.dma_start(out[nb * P : (nb + 1) * P, lo:hi], res[:])
+
         for nb in range(NB):
-            prods = []
-            for g, pos in enumerate((pos1_t, pos2_t)):
-                pr = ring.tile([P, T], F32, name=f"prod{g}")
-                nc.vector.tensor_tensor(pr[:], sums[nb][:].indirect(pos[:]), gates[g][:], MULT)
-                prods.append(pr)
-            res = ring.tile([P, T], F32, name="res")
-            nc.vector.tensor_tensor(res[:], prods[0][:], prods[1][:], ADD)
-            nc.sync.dma_start(out[nb * P : (nb + 1) * P, :], res[:])
+            multiply(nb)
+        waiting = None
+        for nb in range(NB - 1):
+            first = product(nb, 0)
+            if waiting:
+                add(*waiting)
+            second = product(nb, 1)
+            waiting = (nb, first[:], second[:])
+        nb = NB - 1
+        first = product(nb, 0)
+        add(*waiting)
+        halves = [product(nb, 1, lo, lo + H) for lo in (0, H)]
+        for lo, second in zip((0, H), halves):
+            add(nb, first[:, lo : lo + H], second[:], lo, lo + H)

from contextlib import ExitStack

import concourse.mybir as mybir

K, T, E, C, N = 1536, 512, 8, 128, 512
F32 = mybir.dt.float32
BF16 = mybir.dt.bfloat16
I32 = mybir.dt.int32
U32 = mybir.dt.uint32
U16 = mybir.dt.uint16
U8 = mybir.dt.uint8
FP8X4 = mybir.dt.float8_e4m3fn_x4
MULT = mybir.AluOpType.mult
ADD = mybir.AluOpType.add

P = 128
PACK = 4
A = K // (P * PACK)
SLOTS = E * C
NB = N // P
FULL = 2
PARTS = ((2, 4), (4, 6), (6, 8))
GROUPS = ((0, 3), (3, 6), (6, 8))

FLOPS = 2 * K * N * SLOTS
BYTES = 4 * K * T + K * N * E + K * N * E // 32 + 4 * 2 * T + 2 * (8 * SLOTS + 2 * 8 * T) + 4 * N * T


def tile_routed_moe_kernel(tc, xT, w_words, w_scales, gate, offs, pos1, pos2, out):
    nc = tc.nc
    with ExitStack() as ctx:
        keep = ctx.enter_context(tc.tile_pool(name="keep", bufs=1))
        ring = ctx.enter_context(tc.tile_pool(name="ring", bufs=4))
        banks = {}
        for tag, bufs in (("low", 2), ("even", 1), ("odd", 1), ("gate", 2), ("extra", 1)):
            banks[tag] = ctx.enter_context(tc.psum_pool(name=f"psum_{tag}", bufs=bufs))

        offs_t = keep.tile([P, SLOTS // 16], U16, name="offs_t")
        pos1_t = keep.tile([P, T // 16], U16, name="pos1_t")
        pos2_t = keep.tile([P, T // 16], U16, name="pos2_t")

        wsc = keep.tile([P, E, N], U8, name="wsc", align_bytes=64)
        nc.vector.memset(wsc[:].rearrange("p e n -> p (e n)").bitcast(I32), 0)
        xs = keep.tile([P, T], U8, name="xs", align_bytes=64)
        nc.gpsimd.memset(xs[:], 0)
        grow = keep.tile([P, 2, T], F32, name="grow")
        nc.gpsimd.memset(grow[:], 0.0)

        raws = []
        for a in range(A):
            raw = keep.tile([P, PACK, T], F32, name=f"raw{a}")
            raws.append(raw)
        xv = xT.rearrange("(a p j) w -> a p j w", p=P, j=PACK)
        H = T // 2
        for h in range(2):
            nc.sync.dma_start(raws[0][:, :, h * H : (h + 1) * H], xv[0][:, :, h * H : (h + 1) * H])
        nc.sync.dma_start(offs_t[:], offs)
        nc.sync.dma_start(raws[1][:], xv[1])
        nc.sync.dma_start(raws[2][:], xv[2])
        nc.sync.dma_start(grow[0:1, :, :], gate[:, 0:1, :].rearrange("g o t -> o g t"))
        for a in range(A):
            for r in range(4):
                nc.sync.dma_start(
                    wsc[4 * a + r : P : 32, :, :].bitcast(I32),
                    w_scales[:, a, r:16:4, :].bitcast(I32).rearrange("e q n -> q e n"),
                )
        wfull = []
        for e in range(FULL):
            w = keep.tile([P, A, N], U32, name=f"wfull{e}", align_bytes=64)
            nc.sync.dma_start(w[:].bitcast(I32), w_words[e].rearrange("a p n r -> p a (n r)").bitcast(I32))
            wfull.append(w)
        wpart = {}
        for nb in range(NB):
            for lo, hi in PARTS:
                w = keep.tile([P, (hi - lo) * A, P], U32, name=f"wpart{nb}_{lo}", align_bytes=64)
                src = w_words[lo:hi, :, :, nb * P : (nb + 1) * P, :]
                nc.sync.dma_start(w[:].bitcast(I32), src.rearrange("e a p n r -> p (e a) (n r)").bitcast(I32))
                for e in range(lo, hi):
                    wpart[nb, e] = w[:, (e - lo) * A : (e - lo + 1) * A, :]
            if nb == 0:
                nc.sync.dma_start(pos1_t[:], pos1)
                nc.sync.dma_start(pos2_t[:], pos2)

        xq = []
        gq = []
        gs = keep.tile([P, SLOTS], U8, name="gs", align_bytes=64)
        for a in range(A):
            g = keep.tile([P, T, PACK], BF16, name=f"grouped{a}", tag="late" if a == A - 1 else f"grouped{a}", align_bytes=64)
            dst = g[:].rearrange("p (c i) t -> p c t i", i=4)
            src = raws[a][:].rearrange("p t (c i) -> p c t i", i=4)
            q = keep.tile([P, T], U32, name=f"xq{a}", align_bytes=64)

            def quantise(lo, hi):
                nc.vector.quantize_mx(
                    out=q[:, lo:hi].bitcast(FP8X4),
                    scales=xs[4 * a : P, lo:hi],
                    in_=g[:, lo:hi, :].rearrange("p w j -> p (w j)"),
                )

            if a == 0:
                nc.vector.tensor_copy(dst[:, 0:64], src[:, 0:64])
                quantise(0, 256)
                nc.scalar.copy(dst[:, 104:128], src[:, 104:128])
                nc.vector.tensor_copy(dst[:, 64:104], src[:, 64:104])
                quantise(256, 512)
            elif a == 1:
                nc.scalar.copy(dst[:, 48:128], src[:, 48:128])
                nc.vector.tensor_copy(dst[:, 0:48], src[:, 0:48])
                quantise(0, 512)
            else:
                nc.scalar.copy(dst, src)
                quantise(0, 512)
            xq.append(q)
            gathered = keep.tile([P, SLOTS], U32, name=f"gq{a}", align_bytes=64)
            gq.append(gathered)
            for first, last in GROUPS:
                lo, hi = first * C, last * C
                idx = offs_t[:, lo // 16 : hi // 16]
                if a == A - 1:
                    nc.vector.tensor_copy(gs[:, lo:hi], xs[:].indirect(idx))
                nc.vector.tensor_copy(gathered[:, lo:hi], q[:].indirect(idx))

        ones = keep.tile([P, P], F32, name="ones", tag="late", align_bytes=64)
        nc.gpsimd.memset(ones[:], 1.0)
        gates = []
        for g in range(2):
            bank = banks["gate"].tile([P, T], F32, name=f"gbank{g}", tag="gate")
            nc.tensor.matmul(bank[:], lhsT=ones[:], rhs=grow[:, g, :], start=True, stop=True)
            gt = keep.tile([P, T], F32, name=f"gate{g}")
            nc.scalar.copy(gt[:], bank[:])
            gates.append(gt)

        sums = []
        for nb in range(NB):
            ysb = keep.tile([P, SLOTS], F32, name=f"y{nb}")
            sums.append(ysb)

        def one_pass(nb, bank, column, e, a):
            if e < FULL:
                lhs = wfull[e][:, a, nb * P : (nb + 1) * P]
            else:
                lhs = wpart[nb, e][:, a, :]
            nc.tensor.matmul_mx(
                out=bank[:, column : column + C],
                lhsT=lhs.bitcast(FP8X4),
                lhsT_scale=wsc[4 * a : P, e, nb * P : (nb + 1) * P],
                rhs=gq[a][:, e * C : (e + 1) * C].bitcast(FP8X4),
                rhs_scale=gs[4 * a : P, e * C : (e + 1) * C],
                start=(a == 0),
                stop=(a == A - 1),
            )

        def open_bank(tag, name):
            bank = banks[tag].tile([P, T], F32, name=name, tag=tag)
            return bank

        def multiply(nb):
            for i, (first, last) in enumerate(GROUPS):
                tag = "low" if i == 0 else ("even", "odd")[(nb + i + 1) % 2]
                bank = open_bank(tag, f"acc{nb}_{first}")
                if nb == 0 and i == 2:
                    extra = open_bank("extra", "extra")
                    for a in range(A):
                        one_pass(nb, bank, 0, 6, a)
                        one_pass(nb, extra, 0, 7, a)
                    nc.scalar.copy(sums[nb][:, 6 * C : 7 * C], bank[:, :C])
                    nc.vector.tensor_copy(sums[nb][:, 7 * C :], extra[:, :C])
                    continue
                for e in range(first, last):
                    for a in range(A):
                        one_pass(nb, bank, (e - first) * C, e, a)
                nc.scalar.copy(sums[nb][:, first * C : last * C], bank[:, : (last - first) * C])

        def product(nb, g, lo=0, hi=T):
            pr = ring.tile([P, hi - lo], F32, name=f"prod{nb}_{g}_{lo}", tag=f"prod{g}")
            idx = (pos1_t, pos2_t)[g][:, lo // 16 : hi // 16]
            nc.vector.tensor_tensor(pr[:], sums[nb][:].indirect(idx), gates[g][:, lo:hi], MULT)
            return pr

        def add(nb, a, b, lo=0, hi=T):
            res = ring.tile([P, hi - lo], F32, name=f"res{nb}_{lo}", tag="res")
            nc.vector.tensor_tensor(res[:], a, b, ADD)
            nc.sync.dma_start(out[nb * P : (nb + 1) * P, lo:hi], res[:])

        for nb in range(NB):
            multiply(nb)
        waiting = None
        for nb in range(NB - 1):
            first = product(nb, 0)
            if waiting:
                add(*waiting)
            second = product(nb, 1)
            waiting = (nb, first[:], second[:])
        nb = NB - 1
        first = product(nb, 0)
        add(*waiting)
        halves = [product(nb, 1, lo, lo + H) for lo in (0, H)]
        for lo, second in zip((0, H), halves):
            add(nb, first[:, lo : lo + H], second[:], lo, lo + H)
